import numpy as np
import ml_dtypes


def mxq(x, axis, fmt="e4m3"):
    dtype, down = {"e4m3": (ml_dtypes.float8_e4m3fn, 7), "e5m2": (ml_dtypes.float8_e5m2, 14)}[fmt]
    v = np.moveaxis(np.asarray(x, np.float32).astype(ml_dtypes.bfloat16).astype(np.float64), axis, -1)
    blocks = v.reshape(v.shape[:-1] + (-1, 32))
    amax = np.abs(blocks).max(-1, keepdims=True)
    byte = np.maximum(np.where(amax > 0, np.frexp(amax)[1] - 1 + 127, 0) - down, 1)
    scale = np.exp2(byte - 127.0)
    codes = (blocks / scale).astype(np.float32).astype(dtype).astype(np.float64)
    return np.moveaxis((codes * scale).reshape(v.shape), -1, axis)


WIDE = False


def mx_kscale(k):
    if not WIDE:
        return np.ones(k)
    levels = np.array([10, -10, 5, -5, 0])
    if k % 512:
        return np.exp2(np.random.permutation(np.resize(levels, k // 32))).repeat(32)
    a = np.empty((k // 512, 16))
    for p in range(k // 512):
        a[p, :8] = np.random.permutation(np.resize(levels, 8))
        for g in range(8):
            far = levels[np.abs(levels - a[p, g]) >= 10]
            a[p, g + 8] = far[np.random.randint(len(far))]
    return np.exp2(a.ravel()).repeat(32)


def f64(x):
    return np.asarray(x).astype(np.float64)


def striped(idx):
    return np.tile(idx.reshape(-1, 16).T, (8, 1)).astype(np.uint16)


def unstriped(offs):
    return offs[:16].T.reshape(-1).astype(np.int64)


def striped8(idx):
    return np.concatenate([v.reshape(-1, 16).T for v in idx]).astype(np.uint16)


def unstriped8(offs):
    return np.stack([offs[16 * g:16 * g + 16].T.reshape(-1) for g in range(8)]).astype(np.int64)


E2M1 = np.array([0.0, 0.5, 1.0, 1.5, 2.0, 3.0, 4.0, 6.0, -0.0, -0.5, -1.0, -1.5, -2.0, -3.0, -4.0, -6.0])


def pack_weight(w, fmt):
    k, n = w.shape
    w = f64(np.asarray(w, np.float32).astype(ml_dtypes.bfloat16)).reshape(k // 32, 32, n)
    amax = np.abs(w).max(1)
    if fmt == "e4m3":
        byte = np.frexp(amax)[1] - 1 + 127 - 7
    else:
        mant, ex = np.frexp(amax / 6.0)
        byte = np.where(mant > 0.5, ex, ex - 1) + 127
    byte = np.clip(np.where(amax > 0, byte, 1), 1, 254)
    scaled = (w * np.exp2(127.0 - byte)[:, None, :]).reshape(k, n).astype(np.float32)
    by_word = np.ascontiguousarray(scaled.reshape(k // 512, 128, 4, n).transpose(0, 1, 3, 2))
    if fmt == "e4m3":
        words = by_word.astype(ml_dtypes.float8_e4m3fn).view(np.uint8)
    else:
        c = by_word.astype(ml_dtypes.float4_e2m1fn).view(np.uint8) & 0xF
        words = (c[..., 0::2] | (c[..., 1::2] << 4)).reshape(k // 512, 128, 2 * n)
    return np.ascontiguousarray(words), np.ascontiguousarray(byte.astype(np.uint8).reshape(k // 512, 16, n))


def unpack_weight(words, scales, fmt):
    g, _, n = scales.shape
    words = np.ascontiguousarray(words).reshape(g, 128, n, -1)
    if fmt == "e4m3":
        vals = words.view(ml_dtypes.float8_e4m3fn).astype(np.float64)
    else:
        nib = np.empty((g, 128, n, 4), np.uint8)
        nib[..., 0::2] = words & 0xF
        nib[..., 1::2] = words >> 4
        vals = E2M1[nib]
    vals = vals * np.repeat(np.exp2(scales.astype(np.float64) - 127.0), 8, axis=1)[..., None]
    return vals.transpose(0, 1, 3, 2).reshape(g * 512, n)


def pack_table(v):
    words, scales = pack_weight(v, "e4m3")
    return np.concatenate([words.reshape(words.shape[0], -1), scales.reshape(scales.shape[0], -1)], axis=1)


def unpack_table(tab):
    g, t = tab.shape[0], tab.shape[1] // 528
    return unpack_weight(tab[:, :512 * t].reshape(g, 128, t, 4), tab[:, 512 * t:].reshape(g, 16, t), "e4m3")


K, M, T, S = 2048, 128, 1024, 512


def setup_inputs():
    n = np.random.standard_normal
    s = mx_kscale(K)[:, None]
    return {
        "tab": pack_table(n((K, T)) * s),
        "w": (n((K, M)) / np.sqrt(K) / s).astype(np.float32),
        "b": (0.3 * n(128)).astype(np.float32),
        "wgo": np.repeat(np.random.uniform(0.5, 2.0, (8, S)), 16, axis=0).astype(np.float32),
        "offs": striped(np.random.permutation(T)[:S]),
        "offs2": striped8(np.stack([np.random.permutation(T)[:S] for _ in range(8)])),
    }


def reference(tab, w, b, wgo, offs, offs2):
    tab_ = unpack_table(tab)[:, unstriped(offs)]
    w_ = mxq(f64(w), 0, "e4m3")
    y = w_.T @ tab_
    place = unstriped8(offs2)[np.arange(M) % 128 // 16]
    out = np.zeros((M, T))
    out[np.arange(M)[:, None], place] = f64(wgo)[np.arange(M) % 128] * (y + f64(b)[:, None])
    return out

@@ -1,0 +1,107 @@
+import concourse.mybir as mybir
+
+K, M, T, S = 2048, 128, 1024, 512
+FLOPS = 2 * K * M * S
+
+P = 128
+PASSES = K // 512
+HALF = S // 2
+HALF_COLS = HALF // 16
+
+F32 = mybir.dt.float32
+BF16 = mybir.dt.bfloat16
+I32 = mybir.dt.int32
+U32 = mybir.dt.uint32
+U16 = mybir.dt.uint16
+U8 = mybir.dt.uint8
+FP8X4 = mybir.dt.float8_e4m3fn_x4
+IDENTITY = mybir.ActivationFunctionType.Identity
+MULT = mybir.AluOpType.mult
+
+
+def tile_list_tabhs_bias_kernel(tc, tab, w, b, wgo, offs, offs2, out):
+    nc = tc.nc
+    with tc.tile_pool(name="held", bufs=1) as held, tc.psum_pool(name="psum", bufs=1) as psum:
+        picks = held.tile([P, S // 16], U16, name="picks")
+        places = held.tile([P, S // 16], U16, name="places")
+        bias = held.tile([P, 1], F32, name="bias")
+        warm = held.tile([P, 1], F32, name="warm")
+        wgo_sb = held.tile([P, S], F32, name="wgo_sb")
+        scales = held.tile([P, T], U8, name="scales", align_bytes=64)
+        words = [held.tile([P, T], I32, name=f"words{a}", align_bytes=64) for a in range(PASSES)]
+        got_scales = held.tile([P, S], U8, name="got_scales", align_bytes=64)
+        got_words = [held.tile([P, S], U32, name=f"got_words{a}", align_bytes=64) for a in range(PASSES)]
+        w_raw = [held.tile([P, 4, M], F32, name=f"w_raw{a}", align_bytes=64) for a in range(PASSES)]
+        w_bf = [held.tile([P, M, 4], BF16, name=f"w_bf{a}", align_bytes=64) for a in range(PASSES)]
+        w_codes = [held.tile([P, M], U32, name=f"w_codes{a}", align_bytes=64) for a in range(PASSES)]
+        w_scales = [held.tile([P, M], U8, name=f"w_scales{a}", align_bytes=64) for a in range(PASSES)]
+        y = [held.tile([P, HALF], F32, name=f"y{h}") for h in range(2)]
+        placed = held.tile([P, T], F32, name="placed")
+        acc = [psum.tile([P, HALF], F32, name=f"acc{h}") for h in range(2)]
+
+        nc.vector.memset(scales[:].bitcast(I32), 0)
+        nc.vector.memset(warm[:], 0.0)
+        nc.vector.memset(placed[:], 0.0)
+        nc.scalar.activation(out=warm[:], in_=warm[:], func=IDENTITY)
+
+        nc.sync.dma_start(picks[:], offs)
+        nc.sync.dma_start(places[:], offs2)
+        nc.scalar.dma_start(bias[:], b.rearrange("(p o) -> p o", o=1))
+
+        scale_rows = tab[:, 512 * T : 528 * T].rearrange("a (q t) -> a q t", q=16)
+        for quad in range(4):
+            nc.sync.dma_start(
+                scales[32 * quad : 32 * quad + 16, :].bitcast(I32),
+                scale_rows[:, 4 * quad : 4 * quad + 4, :].bitcast(I32),
+            )
+
+        def load_words(a):
+            nc.sync.dma_start(words[a][:], tab[a, 0 : 512 * T].rearrange("(p x) -> p x", p=P).bitcast(I32))
+
+        def load_w(a):
+            nc.sync.dma_start(w_raw[a][:], w[512 * a : 512 * a + 512, :].rearrange("(p j) n -> p j n", j=4))
+
+        def pick(a, lo, hi):
+            nc.vector.tensor_copy(
+                got_words[a][:, 16 * lo : 16 * hi], words[a][:].bitcast(U32).indirect(picks[:, lo:hi])
+            )
+
+        load_words(0)
+        load_words(1)
+        load_words(2)
+        for a in range(PASSES):
+            load_w(a)
+        load_words(3)
+        nc.sync.dma_start(wgo_sb[:], wgo)
+
+        nc.vector.tensor_copy(got_scales[:], scales[:].indirect(picks[:]))
+        for a in range(3):
+            pick(a, 0, 2 * HALF_COLS)
+        for a in range(PASSES):
+            nc.scalar.copy(out=w_bf[a][:], in_=w_raw[a][:].rearrange("p j n -> p n j"))
+            nc.vector.quantize_mx(
+                out=w_codes[a][:].bitcast(FP8X4), scales=w_scales[a][:], in_=w_bf[a][:].rearrange("p n j -> p (n j)")
+            )
+        for h in range(2):
+            pick(3, h * HALF_COLS, (h + 1) * HALF_COLS)
+        for h in range(2):
+            cols = slice(h * HALF, (h + 1) * HALF)
+            for a in range(PASSES):
+                nc.tensor.matmul_mx(
+                    out=acc[h][:],
+                    lhsT=w_codes[a][:].bitcast(FP8X4),
+                    lhsT_scale=w_scales[a][:],
+                    rhs=got_words[a][:, cols].bitcast(FP8X4),
+                    rhs_scale=got_scales[4 * a : P, cols],
+                    start=(a == 0),
+                    stop=(a == PASSES - 1),
+                )
+            nc.scalar.activation(out=y[h][:], in_=acc[h][:], func=IDENTITY, bias=bias[:])
+        for h in range(2):
+            nc.vector.tensor_tensor(
+                placed[:].indirect(places[:, h * HALF_COLS : (h + 1) * HALF_COLS]),
+                y[h][:],
+                wgo_sb[:, h * HALF : (h + 1) * HALF],
+                MULT,
+            )
+        nc.sync.dma_start(out, placed[:])

@@ -31,77 +31,108 @@ def tile_list_tabhs_bias_kernel(tc, tab, w, b, wgo, offs, offs2, out):
         words = [held.tile([P, T], I32, name=f"words{a}", align_bytes=64) for a in range(PASSES)]
         got_scales = held.tile([P, S], U8, name="got_scales", align_bytes=64)
         got_words = [held.tile([P, S], U32, name=f"got_words{a}", align_bytes=64) for a in range(PASSES)]
-        w_raw = [held.tile([P, 4, M], F32, name=f"w_raw{a}", align_bytes=64) for a in range(PASSES)]
-        w_bf = [held.tile([P, M, 4], BF16, name=f"w_bf{a}", align_bytes=64) for a in range(PASSES)]
-        w_codes = [held.tile([P, M], U32, name=f"w_codes{a}", align_bytes=64) for a in range(PASSES)]
-        w_scales = [held.tile([P, M], U8, name=f"w_scales{a}", align_bytes=64) for a in range(PASSES)]
+        w_raw = [held.tile([P, 2, 4, M], F32, name=f"w_raw{u}", align_bytes=64) for u in range(2)]
+        w_bf = [held.tile([P, 2, M, 4], BF16, name=f"w_bf{u}", align_bytes=64) for u in range(2)]
+        w_codes = [held.tile([P, 2 * M], U32, name=f"w_codes{u}", align_bytes=64) for u in range(2)]
+        w_scales = [held.tile([P, 2 * M], U8, name=f"w_scales{u}", align_bytes=64) for u in range(2)]
         y = [held.tile([P, HALF], F32, name=f"y{h}") for h in range(2)]
         placed = held.tile([P, T], F32, name="placed")
         acc = [psum.tile([P, HALF], F32, name=f"acc{h}") for h in range(2)]
 
+        nc.scalar.dma_start(bias[:], b.rearrange("(p o) -> p o", o=1))
         nc.vector.memset(scales[:].bitcast(I32), 0)
         nc.vector.memset(warm[:], 0.0)
         nc.vector.memset(placed[:], 0.0)
         nc.scalar.activation(out=warm[:], in_=warm[:], func=IDENTITY)
 
-        nc.sync.dma_start(picks[:], offs)
-        nc.sync.dma_start(places[:], offs2)
-        nc.scalar.dma_start(bias[:], b.rearrange("(p o) -> p o", o=1))
-
         scale_rows = tab[:, 512 * T : 528 * T].rearrange("a (q t) -> a q t", q=16)
-        for quad in range(4):
-            nc.sync.dma_start(
-                scales[32 * quad : 32 * quad + 16, :].bitcast(I32),
-                scale_rows[:, 4 * quad : 4 * quad + 4, :].bitcast(I32),
-            )
+
+        def load_scales():
+            for quad in range(4):
+                nc.sync.dma_start(
+                    scales[32 * quad : 32 * quad + 16, :].bitcast(I32),
+                    scale_rows[:, 4 * quad : 4 * quad + 4, :].bitcast(I32),
+                )
 
         def load_words(a):
             nc.sync.dma_start(words[a][:], tab[a, 0 : 512 * T].rearrange("(p x) -> p x", p=P).bitcast(I32))
 
         def load_w(a):
-            nc.sync.dma_start(w_raw[a][:], w[512 * a : 512 * a + 512, :].rearrange("(p j) n -> p j n", j=4))
+            u, v = divmod(a, 2)
+            nc.sync.dma_start(w_raw[u][:, v], w[512 * a : 512 * a + 512, :].rearrange("(p j) n -> p j n", j=4))
 
         def pick(a, lo, hi):
             nc.vector.tensor_copy(
                 got_words[a][:, 16 * lo : 16 * hi], words[a][:].bitcast(U32).indirect(picks[:, lo:hi])
             )
 
-        load_words(0)
-        load_words(1)
-        load_words(2)
-        for a in range(PASSES):
-            load_w(a)
-        load_words(3)
-        nc.sync.dma_start(wgo_sb[:], wgo)
+        def interleave(a):
+            u, v = divmod(a, 2)
+            nc.scalar.copy(out=w_bf[u][:, v], in_=w_raw[u][:, v].rearrange("p j n -> p n j"))
 
-        nc.vector.tensor_copy(got_scales[:], scales[:].indirect(picks[:]))
-        for a in range(3):
-            pick(a, 0, 2 * HALF_COLS)
-        for a in range(PASSES):
-            nc.scalar.copy(out=w_bf[a][:], in_=w_raw[a][:].rearrange("p j n -> p n j"))
+        def quantise(u):
             nc.vector.quantize_mx(
-                out=w_codes[a][:].bitcast(FP8X4), scales=w_scales[a][:], in_=w_bf[a][:].rearrange("p n j -> p (n j)")
+                out=w_codes[u][:].bitcast(FP8X4), scales=w_scales[u][:], in_=w_bf[u][:].rearrange("p a n j -> p (a n j)")
             )
-        for h in range(2):
-            pick(3, h * HALF_COLS, (h + 1) * HALF_COLS)
-        for h in range(2):
+
+        def multiply(a, h):
             cols = slice(h * HALF, (h + 1) * HALF)
-            for a in range(PASSES):
-                nc.tensor.matmul_mx(
-                    out=acc[h][:],
-                    lhsT=w_codes[a][:].bitcast(FP8X4),
-                    lhsT_scale=w_scales[a][:],
-                    rhs=got_words[a][:, cols].bitcast(FP8X4),
-                    rhs_scale=got_scales[4 * a : P, cols],
-                    start=(a == 0),
-                    stop=(a == PASSES - 1),
-                )
+            u, v = divmod(a, 2)
+            nc.tensor.matmul_mx(
+                out=acc[h][:],
+                lhsT=w_codes[u][:, v * M : (v + 1) * M].bitcast(FP8X4),
+                lhsT_scale=w_scales[u][:, v * M : (v + 1) * M],
+                rhs=got_words[a][:, cols].bitcast(FP8X4),
+                rhs_scale=got_scales[4 * a : P, cols],
+                start=(a == 0),
+                stop=(a == PASSES - 1),
+            )
+
+        def add_bias(h):
             nc.scalar.activation(out=y[h][:], in_=acc[h][:], func=IDENTITY, bias=bias[:])
-        for h in range(2):
+
+        def place(h):
             nc.vector.tensor_tensor(
                 placed[:].indirect(places[:, h * HALF_COLS : (h + 1) * HALF_COLS]),
                 y[h][:],
                 wgo_sb[:, h * HALF : (h + 1) * HALF],
                 MULT,
             )
+
+        nc.sync.dma_start(picks[:], offs)
+        load_words(0)
+        load_words(1)
+        load_scales()
+        load_w(0)
+        load_w(1)
+        load_words(2)
+        load_w(2)
+        load_w(3)
+        load_words(3)
+        nc.sync.dma_start(places[:], offs2)
+        nc.sync.dma_start(wgo_sb[:], wgo)
+        pick(0, 0, 2 * HALF_COLS)
+        pick(1, 0, 2 * HALF_COLS)
+        nc.vector.tensor_copy(got_scales[:], scales[:].indirect(picks[:]))
+        interleave(0)
+        interleave(1)
+        quantise(0)
+        multiply(0, 0)
+        multiply(1, 0)
+        multiply(0, 1)
+        multiply(1, 1)
+        pick(2, 0, 2 * HALF_COLS)
+        interleave(2)
+        interleave(3)
+        quantise(1)
+        multiply(2, 0)
+        multiply(2, 1)
+        pick(3, 0, HALF_COLS)
+        multiply(3, 0)
+        add_bias(0)
+        pick(3, HALF_COLS, 2 * HALF_COLS)
+        multiply(3, 1)
+        add_bias(1)
+        place(0)
+        place(1)
         nc.sync.dma_start(out, placed[:])

@@ -7,6 +7,7 @@ P = 128
 PASSES = K // 512
 HALF = S // 2
 HALF_COLS = HALF // 16
+CUTS = ((0, 128), (128, 256), (256, 512))
 
 F32 = mybir.dt.float32
 BF16 = mybir.dt.bfloat16
@@ -30,16 +31,16 @@ def tile_list_tabhs_bias_kernel(tc, tab, w, b, wgo, offs, offs2, out):
         scales = held.tile([P, T], U8, name="scales", align_bytes=64)
         words = [held.tile([P, T], I32, name=f"words{a}", align_bytes=64) for a in range(PASSES)]
         got_scales = held.tile([P, S], U8, name="got_scales", align_bytes=64)
-        got_words = [held.tile([P, S], U32, name=f"got_words{a}", align_bytes=64) for a in range(PASSES)]
+        got_words = [held.tile([P, S], U32, name=f"got_words{a}", align_bytes=64) for a in range(3)]
+        got_last = [held.tile([P, hi - lo], U32, name=f"got_last{c}", align_bytes=64) for c, (lo, hi) in enumerate(CUTS)]
         w_raw = [held.tile([P, 2, 4, M], F32, name=f"w_raw{u}", align_bytes=64) for u in range(2)]
         w_bf = [held.tile([P, 2, M, 4], BF16, name=f"w_bf{u}", align_bytes=64) for u in range(2)]
         w_codes = [held.tile([P, 2 * M], U32, name=f"w_codes{u}", align_bytes=64) for u in range(2)]
         w_scales = [held.tile([P, 2 * M], U8, name=f"w_scales{u}", align_bytes=64) for u in range(2)]
         y = [held.tile([P, HALF], F32, name=f"y{h}") for h in range(2)]
         placed = held.tile([P, T], F32, name="placed")
-        acc = [psum.tile([P, HALF], F32, name=f"acc{h}") for h in range(2)]
+        acc = [psum.tile([P, hi - lo], F32, name=f"acc{c}") for c, (lo, hi) in enumerate(CUTS)]
 
-        nc.scalar.dma_start(bias[:], b.rearrange("(p o) -> p o", o=1))
         nc.vector.memset(scales[:].bitcast(I32), 0)
         nc.vector.memset(warm[:], 0.0)
         nc.vector.memset(placed[:], 0.0)
@@ -61,9 +62,13 @@ def tile_list_tabhs_bias_kernel(tc, tab, w, b, wgo, offs, offs2, out):
             u, v = divmod(a, 2)
             nc.sync.dma_start(w_raw[u][:, v], w[512 * a : 512 * a + 512, :].rearrange("(p j) n -> p j n", j=4))
 
-        def pick(a, lo, hi):
+        def pick(a):
+            nc.vector.tensor_copy(got_words[a][:], words[a][:].bitcast(U32).indirect(picks[:]))
+
+        def pick_last(c):
+            lo, hi = CUTS[c]
             nc.vector.tensor_copy(
-                got_words[a][:, 16 * lo : 16 * hi], words[a][:].bitcast(U32).indirect(picks[:, lo:hi])
+                got_last[c][:], words[3][:].bitcast(U32).indirect(picks[:, lo // 16 : hi // 16])
             )
 
         def interleave(a):
@@ -75,21 +80,26 @@ def tile_list_tabhs_bias_kernel(tc, tab, w, b, wgo, offs, offs2, out):
                 out=w_codes[u][:].bitcast(FP8X4), scales=w_scales[u][:], in_=w_bf[u][:].rearrange("p a n j -> p (a n j)")
             )
 
-        def multiply(a, h):
-            cols = slice(h * HALF, (h + 1) * HALF)
+        def multiply(a, c):
+            cols = slice(*CUTS[c])
             u, v = divmod(a, 2)
+            got = got_words[a][:, cols] if a < 3 else got_last[c][:]
             nc.tensor.matmul_mx(
-                out=acc[h][:],
+                out=acc[c][:],
                 lhsT=w_codes[u][:, v * M : (v + 1) * M].bitcast(FP8X4),
                 lhsT_scale=w_scales[u][:, v * M : (v + 1) * M],
-                rhs=got_words[a][:, cols].bitcast(FP8X4),
+                rhs=got.bitcast(FP8X4),
                 rhs_scale=got_scales[4 * a : P, cols],
                 start=(a == 0),
                 stop=(a == PASSES - 1),
             )
 
-        def add_bias(h):
-            nc.scalar.activation(out=y[h][:], in_=acc[h][:], func=IDENTITY, bias=bias[:])
+        def add_bias(c):
+            lo, hi = CUTS[c]
+            h = lo // HALF
+            nc.scalar.activation(
+                out=y[h][:, lo - h * HALF : hi - h * HALF], in_=acc[c][:], func=IDENTITY, bias=bias[:]
+            )
 
         def place(h):
             nc.vector.tensor_tensor(
@@ -101,38 +111,34 @@ def tile_list_tabhs_bias_kernel(tc, tab, w, b, wgo, offs, offs2, out):
 
         nc.sync.dma_start(picks[:], offs)
         load_words(0)
-        load_words(1)
         load_scales()
+        load_words(1)
         load_w(0)
         load_w(1)
-        load_words(2)
         load_w(2)
+        load_words(2)
         load_w(3)
         load_words(3)
+        nc.sync.dma_start(bias[:], b.rearrange("(p o) -> p o", o=1))
         nc.sync.dma_start(places[:], offs2)
         nc.sync.dma_start(wgo_sb[:], wgo)
-        pick(0, 0, 2 * HALF_COLS)
-        pick(1, 0, 2 * HALF_COLS)
+        pick(0)
         nc.vector.tensor_copy(got_scales[:], scales[:].indirect(picks[:]))
-        interleave(0)
-        interleave(1)
+        pick(1)
+        for a in range(PASSES):
+            interleave(a)
         quantise(0)
-        multiply(0, 0)
-        multiply(1, 0)
-        multiply(0, 1)
-        multiply(1, 1)
-        pick(2, 0, 2 * HALF_COLS)
-        interleave(2)
-        interleave(3)
+        for c in range(3):
+            multiply(0, c)
+            multiply(1, c)
+        pick(2)
         quantise(1)
-        multiply(2, 0)
-        multiply(2, 1)
-        pick(3, 0, HALF_COLS)
-        multiply(3, 0)
-        add_bias(0)
-        pick(3, HALF_COLS, 2 * HALF_COLS)
-        multiply(3, 1)
-        add_bias(1)
+        for c in range(3):
+            multiply(2, c)
+        for c in range(3):
+            pick_last(c)
+            multiply(3, c)
+            add_bias(c)
         place(0)
         place(1)
         nc.sync.dma_start(out, placed[:])

@@ -41,6 +41,11 @@ def tile_list_tabhs_bias_kernel(tc, tab, w, b, wgo, offs, offs2, out):
         placed = held.tile([P, T], F32, name="placed")
         acc = [psum.tile([P, hi - lo], F32, name=f"acc{c}") for c, (lo, hi) in enumerate(CUTS)]
 
+        def load_words(a, queue):
+            queue.dma_start(words[a][:], tab[a, 0 : 512 * T].rearrange("(p x) -> p x", p=P).bitcast(I32))
+
+        load_words(0, nc.scalar)
+        nc.sync.dma_start(picks[:], offs)
         nc.vector.memset(scales[:].bitcast(I32), 0)
         nc.vector.memset(warm[:], 0.0)
         nc.vector.memset(placed[:], 0.0)
@@ -54,9 +59,6 @@ def tile_list_tabhs_bias_kernel(tc, tab, w, b, wgo, offs, offs2, out):
                     scales[32 * quad : 32 * quad + 16, :].bitcast(I32),
                     scale_rows[:, 4 * quad : 4 * quad + 4, :].bitcast(I32),
                 )
-
-        def load_words(a):
-            nc.sync.dma_start(words[a][:], tab[a, 0 : 512 * T].rearrange("(p x) -> p x", p=P).bitcast(I32))
 
         def load_w(a):
             u, v = divmod(a, 2)
@@ -109,22 +111,20 @@ def tile_list_tabhs_bias_kernel(tc, tab, w, b, wgo, offs, offs2, out):
                 MULT,
             )
 
-        nc.sync.dma_start(picks[:], offs)
-        load_words(0)
         load_scales()
-        load_words(1)
+        load_words(1, nc.sync)
         load_w(0)
         load_w(1)
         load_w(2)
-        load_words(2)
+        load_words(2, nc.sync)
         load_w(3)
-        load_words(3)
+        load_words(3, nc.sync)
         nc.sync.dma_start(bias[:], b.rearrange("(p o) -> p o", o=1))
         nc.sync.dma_start(places[:], offs2)
         nc.sync.dma_start(wgo_sb[:], wgo)
         pick(0)
-        nc.vector.tensor_copy(got_scales[:], scales[:].indirect(picks[:]))
         pick(1)
+        nc.vector.tensor_copy(got_scales[:], scales[:].indirect(picks[:]))
         for a in range(PASSES):
             interleave(a)
         quantise(0)

@@ -4,10 +4,15 @@ K, M, T, S = 2048, 128, 1024, 512
 FLOPS = 2 * K * M * S
 
 P = 128
-PASSES = K // 512
+PACK = 4
+K_PASS = P * PACK
+PASSES = K // K_PASS
+LAST = PASSES - 1
+SCALE_ROWS = K_PASS // 32
+PER_OFFSET_COLUMN = 16
 HALF = S // 2
-HALF_COLS = HALF // 16
-CUTS = ((0, 128), (128, 256), (256, 512))
+
+CHUNKS = ((0, 128), (128, 256), (256, 512))
 
 F32 = mybir.dt.float32
 BF16 = mybir.dt.bfloat16
@@ -23,26 +28,86 @@ MULT = mybir.AluOpType.mult
 def tile_list_tabhs_bias_kernel(tc, tab, w, b, wgo, offs, offs2, out):
     nc = tc.nc
     with tc.tile_pool(name="held", bufs=1) as held, tc.psum_pool(name="psum", bufs=1) as psum:
-        picks = held.tile([P, S // 16], U16, name="picks")
-        places = held.tile([P, S // 16], U16, name="places")
+        picks = held.tile([P, S // PER_OFFSET_COLUMN], U16, name="picks")
+        places = held.tile([P, S // PER_OFFSET_COLUMN], U16, name="places")
         bias = held.tile([P, 1], F32, name="bias")
         warm = held.tile([P, 1], F32, name="warm")
-        wgo_sb = held.tile([P, S], F32, name="wgo_sb")
+        weights_out = held.tile([P, S], F32, name="weights_out")
         scales = held.tile([P, T], U8, name="scales", align_bytes=64)
+        picked_scales = held.tile([P, S], U8, name="picked_scales", align_bytes=64)
         words = [held.tile([P, T], I32, name=f"words{a}", align_bytes=64) for a in range(PASSES)]
-        got_scales = held.tile([P, S], U8, name="got_scales", align_bytes=64)
-        got_words = [held.tile([P, S], U32, name=f"got_words{a}", align_bytes=64) for a in range(3)]
-        got_last = [held.tile([P, hi - lo], U32, name=f"got_last{c}", align_bytes=64) for c, (lo, hi) in enumerate(CUTS)]
-        w_raw = [held.tile([P, 2, 4, M], F32, name=f"w_raw{u}", align_bytes=64) for u in range(2)]
-        w_bf = [held.tile([P, 2, M, 4], BF16, name=f"w_bf{u}", align_bytes=64) for u in range(2)]
-        w_codes = [held.tile([P, 2 * M], U32, name=f"w_codes{u}", align_bytes=64) for u in range(2)]
-        w_scales = [held.tile([P, 2 * M], U8, name=f"w_scales{u}", align_bytes=64) for u in range(2)]
+        picked_words = [held.tile([P, S], U32, name=f"picked_words{a}", align_bytes=64) for a in range(LAST)]
+        picked_last = [
+            held.tile([P, hi - lo], U32, name=f"picked_last{c}", align_bytes=64) for c, (lo, hi) in enumerate(CHUNKS)
+        ]
+        w_raw = [held.tile([P, 2, PACK, M], F32, name=f"w_raw{u}", align_bytes=64) for u in range(PASSES // 2)]
+        w_grouped = [held.tile([P, 2, M, PACK], BF16, name=f"w_grouped{u}", align_bytes=64) for u in range(PASSES // 2)]
+        w_codes = [held.tile([P, 2 * M], U32, name=f"w_codes{u}", align_bytes=64) for u in range(PASSES // 2)]
+        w_scales = [held.tile([P, 2 * M], U8, name=f"w_scales{u}", align_bytes=64) for u in range(PASSES // 2)]
         y = [held.tile([P, HALF], F32, name=f"y{h}") for h in range(2)]
         placed = held.tile([P, T], F32, name="placed")
-        acc = [psum.tile([P, hi - lo], F32, name=f"acc{c}") for c, (lo, hi) in enumerate(CUTS)]
+        sums = [psum.tile([P, hi - lo], F32, name=f"sums{c}") for c, (lo, hi) in enumerate(CHUNKS)]
+
+        scale_rows = tab[:, K_PASS * T :].rearrange("a (q t) -> a q t", q=SCALE_ROWS)
 
         def load_words(a, queue):
-            queue.dma_start(words[a][:], tab[a, 0 : 512 * T].rearrange("(p x) -> p x", p=P).bitcast(I32))
+            queue.dma_start(words[a][:], tab[a, 0 : K_PASS * T].rearrange("(p x) -> p x", p=P).bitcast(I32))
+
+        def load_scales(quadrant):
+            nc.sync.dma_start(
+                scales[32 * quadrant : 32 * quadrant + 16, :].bitcast(I32),
+                scale_rows[:, 4 * quadrant : 4 * quadrant + 4, :].bitcast(I32),
+            )
+
+        def load_w(a):
+            rows = w[K_PASS * a : K_PASS * (a + 1), :]
+            nc.sync.dma_start(w_raw[a // 2][:, a % 2], rows.rearrange("(p j) n -> p j n", j=PACK))
+
+        def offsets(lists, lo, hi):
+            return lists[:, lo // PER_OFFSET_COLUMN : hi // PER_OFFSET_COLUMN]
+
+        def pick_words(target, a, lo, hi):
+            nc.vector.tensor_copy(target[:], words[a][:].bitcast(U32).indirect(offsets(picks, lo, hi)))
+
+        def group_w(a):
+            nc.scalar.copy(out=w_grouped[a // 2][:, a % 2], in_=w_raw[a // 2][:, a % 2].rearrange("p j n -> p n j"))
+
+        def quantise_w(first, count):
+            u, v = divmod(first, 2)
+            cols = slice(v * M, (v + count) * M)
+            nc.vector.quantize_mx(
+                out=w_codes[u][:, cols].bitcast(FP8X4),
+                scales=w_scales[u][:, cols],
+                in_=w_grouped[u][:, v : v + count].rearrange("p a n j -> p (a n j)"),
+            )
+
+        def multiply(a, c):
+            u, v = divmod(a, 2)
+            w_cols = slice(v * M, (v + 1) * M)
+            cols = slice(*CHUNKS[c])
+            moving = picked_last[c][:] if a == LAST else picked_words[a][:, cols]
+            nc.tensor.matmul_mx(
+                out=sums[c][:],
+                lhsT=w_codes[u][:, w_cols].bitcast(FP8X4),
+                lhsT_scale=w_scales[u][:, w_cols],
+                rhs=moving.bitcast(FP8X4),
+                rhs_scale=picked_scales[4 * a :, cols],
+                start=(a == 0),
+                stop=(a == LAST),
+            )
+
+        def add_bias(c):
+            lo, hi = CHUNKS[c]
+            h = lo // HALF
+            nc.scalar.activation(
+                out=y[h][:, lo - h * HALF : hi - h * HALF], in_=sums[c][:], func=IDENTITY, bias=bias[:]
+            )
+
+        def place(h):
+            lo, hi = h * HALF, (h + 1) * HALF
+            nc.vector.tensor_tensor(
+                placed[:].indirect(offsets(places, lo, hi)), y[h][:], weights_out[:, lo:hi], MULT
+            )
 
         load_words(0, nc.scalar)
         nc.sync.dma_start(picks[:], offs)
@@ -50,68 +115,9 @@ def tile_list_tabhs_bias_kernel(tc, tab, w, b, wgo, offs, offs2, out):
         nc.vector.memset(warm[:], 0.0)
         nc.vector.memset(placed[:], 0.0)
         nc.scalar.activation(out=warm[:], in_=warm[:], func=IDENTITY)
+        for quadrant in range(P // 32):
+            load_scales(quadrant)
 
-        scale_rows = tab[:, 512 * T : 528 * T].rearrange("a (q t) -> a q t", q=16)
-
-        def load_scales():
-            for quad in range(4):
-                nc.sync.dma_start(
-                    scales[32 * quad : 32 * quad + 16, :].bitcast(I32),
-                    scale_rows[:, 4 * quad : 4 * quad + 4, :].bitcast(I32),
-                )
-
-        def load_w(a):
-            u, v = divmod(a, 2)
-            nc.sync.dma_start(w_raw[u][:, v], w[512 * a : 512 * a + 512, :].rearrange("(p j) n -> p j n", j=4))
-
-        def pick(a):
-            nc.vector.tensor_copy(got_words[a][:], words[a][:].bitcast(U32).indirect(picks[:]))
-
-        def pick_last(c):
-            lo, hi = CUTS[c]
-            nc.vector.tensor_copy(
-                got_last[c][:], words[3][:].bitcast(U32).indirect(picks[:, lo // 16 : hi // 16])
-            )
-
-        def interleave(a):
-            u, v = divmod(a, 2)
-            nc.scalar.copy(out=w_bf[u][:, v], in_=w_raw[u][:, v].rearrange("p j n -> p n j"))
-
-        def quantise(u):
-            nc.vector.quantize_mx(
-                out=w_codes[u][:].bitcast(FP8X4), scales=w_scales[u][:], in_=w_bf[u][:].rearrange("p a n j -> p (a n j)")
-            )
-
-        def multiply(a, c):
-            cols = slice(*CUTS[c])
-            u, v = divmod(a, 2)
-            got = got_words[a][:, cols] if a < 3 else got_last[c][:]
-            nc.tensor.matmul_mx(
-                out=acc[c][:],
-                lhsT=w_codes[u][:, v * M : (v + 1) * M].bitcast(FP8X4),
-                lhsT_scale=w_scales[u][:, v * M : (v + 1) * M],
-                rhs=got.bitcast(FP8X4),
-                rhs_scale=got_scales[4 * a : P, cols],
-                start=(a == 0),
-                stop=(a == PASSES - 1),
-            )
-
-        def add_bias(c):
-            lo, hi = CUTS[c]
-            h = lo // HALF
-            nc.scalar.activation(
-                out=y[h][:, lo - h * HALF : hi - h * HALF], in_=acc[c][:], func=IDENTITY, bias=bias[:]
-            )
-
-        def place(h):
-            nc.vector.tensor_tensor(
-                placed[:].indirect(places[:, h * HALF_COLS : (h + 1) * HALF_COLS]),
-                y[h][:],
-                wgo_sb[:, h * HALF : (h + 1) * HALF],
-                MULT,
-            )
-
-        load_scales()
         load_words(1, nc.sync)
         load_w(0)
         load_w(1)
@@ -121,23 +127,25 @@ def tile_list_tabhs_bias_kernel(tc, tab, w, b, wgo, offs, offs2, out):
         load_words(3, nc.sync)
         nc.sync.dma_start(bias[:], b.rearrange("(p o) -> p o", o=1))
         nc.sync.dma_start(places[:], offs2)
-        nc.sync.dma_start(wgo_sb[:], wgo)
-        pick(0)
-        pick(1)
-        nc.vector.tensor_copy(got_scales[:], scales[:].indirect(picks[:]))
+        nc.sync.dma_start(weights_out[:], wgo)
+
+        pick_words(picked_words[0], 0, 0, S)
+        pick_words(picked_words[1], 1, 0, S)
+        nc.vector.tensor_copy(picked_scales[:], scales[:].indirect(picks[:]))
         for a in range(PASSES):
-            interleave(a)
-        quantise(0)
-        for c in range(3):
+            group_w(a)
+        quantise_w(0, 2)
+        for c in range(len(CHUNKS)):
             multiply(0, c)
             multiply(1, c)
-        pick(2)
-        quantise(1)
-        for c in range(3):
+        quantise_w(2, 1)
+        pick_words(picked_words[2], 2, 0, S)
+        quantise_w(3, 1)
+        for c in range(len(CHUNKS)):
             multiply(2, c)
-        for c in range(3):
-            pick_last(c)
-            multiply(3, c)
+        for c, (lo, hi) in enumerate(CHUNKS):
+            pick_words(picked_last[c], LAST, lo, hi)
+            multiply(LAST, c)
             add_bias(c)
         place(0)
         place(1)

import concourse.mybir as mybir

K, M, T, S = 2048, 128, 1024, 512
FLOPS = 2 * K * M * S

P = 128
PACK = 4
K_PASS = P * PACK
PASSES = K // K_PASS
LAST = PASSES - 1
SCALE_ROWS = K_PASS // 32
PER_OFFSET_COLUMN = 16
HALF = S // 2

CHUNKS = ((0, 128), (128, 256), (256, 512))

F32 = mybir.dt.float32
BF16 = mybir.dt.bfloat16
I32 = mybir.dt.int32
U32 = mybir.dt.uint32
U16 = mybir.dt.uint16
U8 = mybir.dt.uint8
FP8X4 = mybir.dt.float8_e4m3fn_x4
IDENTITY = mybir.ActivationFunctionType.Identity
MULT = mybir.AluOpType.mult


def tile_list_tabhs_bias_kernel(tc, tab, w, b, wgo, offs, offs2, out):
    nc = tc.nc
    with tc.tile_pool(name="held", bufs=1) as held, tc.psum_pool(name="psum", bufs=1) as psum:
        picks = held.tile([P, S // PER_OFFSET_COLUMN], U16, name="picks")
        places = held.tile([P, S // PER_OFFSET_COLUMN], U16, name="places")
        bias = held.tile([P, 1], F32, name="bias")
        warm = held.tile([P, 1], F32, name="warm")
        weights_out = held.tile([P, S], F32, name="weights_out")
        scales = held.tile([P, T], U8, name="scales", align_bytes=64)
        picked_scales = held.tile([P, S], U8, name="picked_scales", align_bytes=64)
        words = [held.tile([P, T], I32, name=f"words{a}", align_bytes=64) for a in range(PASSES)]
        picked_words = [held.tile([P, S], U32, name=f"picked_words{a}", align_bytes=64) for a in range(LAST)]
        picked_last = [
            held.tile([P, hi - lo], U32, name=f"picked_last{c}", align_bytes=64) for c, (lo, hi) in enumerate(CHUNKS)
        ]
        w_raw = [held.tile([P, 2, PACK, M], F32, name=f"w_raw{u}", align_bytes=64) for u in range(PASSES // 2)]
        w_grouped = [held.tile([P, 2, M, PACK], BF16, name=f"w_grouped{u}", align_bytes=64) for u in range(PASSES // 2)]
        w_codes = [held.tile([P, 2 * M], U32, name=f"w_codes{u}", align_bytes=64) for u in range(PASSES // 2)]
        w_scales = [held.tile([P, 2 * M], U8, name=f"w_scales{u}", align_bytes=64) for u in range(PASSES // 2)]
        y = [held.tile([P, HALF], F32, name=f"y{h}") for h in range(2)]
        placed = held.tile([P, T], F32, name="placed")
        sums = [psum.tile([P, hi - lo], F32, name=f"sums{c}") for c, (lo, hi) in enumerate(CHUNKS)]

        scale_rows = tab[:, K_PASS * T :].rearrange("a (q t) -> a q t", q=SCALE_ROWS)

        def load_words(a, queue):
            queue.dma_start(words[a][:], tab[a, 0 : K_PASS * T].rearrange("(p x) -> p x", p=P).bitcast(I32))

        def load_scales(quadrant):
            nc.sync.dma_start(
                scales[32 * quadrant : 32 * quadrant + 16, :].bitcast(I32),
                scale_rows[:, 4 * quadrant : 4 * quadrant + 4, :].bitcast(I32),
            )

        def load_w(a):
            rows = w[K_PASS * a : K_PASS * (a + 1), :]
            nc.sync.dma_start(w_raw[a // 2][:, a % 2], rows.rearrange("(p j) n -> p j n", j=PACK))

        def offsets(lists, lo, hi):
            return lists[:, lo // PER_OFFSET_COLUMN : hi // PER_OFFSET_COLUMN]

        def pick_words(target, a, lo, hi):
            nc.vector.tensor_copy(target[:], words[a][:].bitcast(U32).indirect(offsets(picks, lo, hi)))

        def group_w(a):
            nc.scalar.copy(out=w_grouped[a // 2][:, a % 2], in_=w_raw[a // 2][:, a % 2].rearrange("p j n -> p n j"))

        def quantise_w(first, count):
            u, v = divmod(first, 2)
            cols = slice(v * M, (v + count) * M)
            nc.vector.quantize_mx(
                out=w_codes[u][:, cols].bitcast(FP8X4),
                scales=w_scales[u][:, cols],
                in_=w_grouped[u][:, v : v + count].rearrange("p a n j -> p (a n j)"),
            )

        def multiply(a, c):
            u, v = divmod(a, 2)
            w_cols = slice(v * M, (v + 1) * M)
            cols = slice(*CHUNKS[c])
            moving = picked_last[c][:] if a == LAST else picked_words[a][:, cols]
            nc.tensor.matmul_mx(
                out=sums[c][:],
                lhsT=w_codes[u][:, w_cols].bitcast(FP8X4),
                lhsT_scale=w_scales[u][:, w_cols],
                rhs=moving.bitcast(FP8X4),
                rhs_scale=picked_scales[4 * a :, cols],
                start=(a == 0),
                stop=(a == LAST),
            )

        def add_bias(c):
            lo, hi = CHUNKS[c]
            h = lo // HALF
            nc.scalar.activation(
                out=y[h][:, lo - h * HALF : hi - h * HALF], in_=sums[c][:], func=IDENTITY, bias=bias[:]
            )

        def place(h):
            lo, hi = h * HALF, (h + 1) * HALF
            nc.vector.tensor_tensor(
                placed[:].indirect(offsets(places, lo, hi)), y[h][:], weights_out[:, lo:hi], MULT
            )

        load_words(0, nc.scalar)
        nc.sync.dma_start(picks[:], offs)
        nc.vector.memset(scales[:].bitcast(I32), 0)
        nc.vector.memset(warm[:], 0.0)
        nc.vector.memset(placed[:], 0.0)
        nc.scalar.activation(out=warm[:], in_=warm[:], func=IDENTITY)
        for quadrant in range(P // 32):
            load_scales(quadrant)

        load_words(1, nc.sync)
        load_w(0)
        load_w(1)
        load_w(2)
        load_words(2, nc.sync)
        load_w(3)
        load_words(3, nc.sync)
        nc.sync.dma_start(bias[:], b.rearrange("(p o) -> p o", o=1))
        nc.sync.dma_start(places[:], offs2)
        nc.sync.dma_start(weights_out[:], wgo)

        pick_words(picked_words[0], 0, 0, S)
        pick_words(picked_words[1], 1, 0, S)
        nc.vector.tensor_copy(picked_scales[:], scales[:].indirect(picks[:]))
        for a in range(PASSES):
            group_w(a)
        quantise_w(0, 2)
        for c in range(len(CHUNKS)):
            multiply(0, c)
            multiply(1, c)
        quantise_w(2, 1)
        pick_words(picked_words[2], 2, 0, S)
        quantise_w(3, 1)
        for c in range(len(CHUNKS)):
            multiply(2, c)
        for c, (lo, hi) in enumerate(CHUNKS):
            pick_words(picked_last[c], LAST, lo, hi)
            multiply(LAST, c)
            add_bias(c)
        place(0)
        place(1)
        nc.sync.dma_start(out, placed[:])
